import numpy as np
import ml_dtypes


def mxq(x, axis, fmt="e4m3"):
    dtype, down = {"e4m3": (ml_dtypes.float8_e4m3fn, 7), "e5m2": (ml_dtypes.float8_e5m2, 14)}[fmt]
    v = np.moveaxis(np.asarray(x, np.float32).astype(ml_dtypes.bfloat16).astype(np.float64), axis, -1)
    blocks = v.reshape(v.shape[:-1] + (-1, 32))
    amax = np.abs(blocks).max(-1, keepdims=True)
    byte = np.maximum(np.where(amax > 0, np.frexp(amax)[1] - 1 + 127, 0) - down, 1)
    scale = np.exp2(byte - 127.0)
    codes = (blocks / scale).astype(np.float32).astype(dtype).astype(np.float64)
    return np.moveaxis((codes * scale).reshape(v.shape), -1, axis)


WIDE = False


def mx_kscale(k):
    if not WIDE:
        return np.ones(k)
    levels = np.array([10, -10, 5, -5, 0])
    if k % 512:
        return np.exp2(np.random.permutation(np.resize(levels, k // 32))).repeat(32)
    a = np.empty((k // 512, 16))
    for p in range(k // 512):
        a[p, :8] = np.random.permutation(np.resize(levels, 8))
        for g in range(8):
            far = levels[np.abs(levels - a[p, g]) >= 10]
            a[p, g + 8] = far[np.random.randint(len(far))]
    return np.exp2(a.ravel()).repeat(32)


def f64(x):
    return np.asarray(x).astype(np.float64)


def striped(idx):
    return np.tile(idx.reshape(-1, 16).T, (8, 1)).astype(np.uint16)


def unstriped(offs):
    return offs[:16].T.reshape(-1).astype(np.int64)


def sigmoid(v):
    return 1.0 / (1.0 + np.exp(-np.maximum(v, -700.0)))


K, T, E, C, H, N = 1536, 512, 2, 256, 512, 384


def by_expert(wq, xq):
    return np.concatenate([wq[e].T @ xq[:, e * C:(e + 1) * C] for e in range(E)], axis=1)


def setup_inputs():
    n = np.random.standard_normal
    s = mx_kscale(K)[:, None]
    u = mx_kscale(H)
    return {
        "xT": (n((K, T)) * s).astype(np.float32),
        "w1": (n((E, K, H)) / np.sqrt(K) / s[None]).astype(np.float32),
        "w3": (n((E, K, H)) / np.sqrt(K) / s[None] * u[None, None, :]).astype(np.float32),
        "w2": (n((E, H, N)) / np.sqrt(H) / u[None, :, None]).astype(np.float32),
        "gate": np.tile(np.random.uniform(0.2, 1.0, E * C), (N, 1)).astype(np.float32),
        "offs": striped(np.random.permutation(T)[:E * C]),
    }


def reference(xT, w1, w3, w2, gate, offs):
    idx = unstriped(offs)
    xq = mxq(f64(xT)[:, idx], 0, "e4m3")
    h = sigmoid(by_expert(mxq(f64(w1), 1, "e4m3"), xq))
    h = h * by_expert(mxq(f64(w3), 1, "e4m3"), xq)
    y = by_expert(mxq(f64(w2), 1, "e4m3"), mxq(h, 0, "e4m3"))
    out = np.zeros((N, T))
    out[:, idx] = f64(gate) * y
    return out

@@ -1,0 +1,301 @@
+from contextlib import ExitStack
+
+import concourse.mybir as mybir
+
+K, T, E, C, H, N = 1536, 512, 2, 256, 512, 384
+FLOPS = 2 * 2 * K * H * T + 2 * H * N * T
+
+F32 = mybir.dt.float32
+BF16 = mybir.dt.bfloat16
+U32 = mybir.dt.uint32
+U16 = mybir.dt.uint16
+U8 = mybir.dt.uint8
+FP8X4 = mybir.dt.float8_e4m3fn_x4
+MULT = mybir.AluOpType.mult
+SIGMOID = mybir.ActivationFunctionType.Sigmoid
+
+P = 128
+PASSES = K // 512
+HALF = 128
+BLOCKS = N // P
+S_X = [208,272,480]
+S_WEIGHTS = [[96,16,72],[64,16,24],[88,104,128],[128,80,40]]
+S_DOWN = [256,256]
+LAST_CUT = 96
+LAST_S = [32,104]
+LAST_QUANTS = 1
+SCATTER_AFTER = [8,8,10]
+SC0 = 256
+SC1 = 256
+HID_ENGINES = [["V","S"],["V","S"]]
+
+
+def share(lo, cut, hi):
+    return [(engine, a, b) for engine, a, b in (("S", lo, cut), ("V", cut, hi)) if a < b]
+
+
+def tile_routed_moe_kernel(tc, xT, w1, w3, w2, gate, offs, out):
+    nc = tc.nc
+    with ExitStack() as ctx:
+        keep = ctx.enter_context(tc.tile_pool(name="keep", bufs=1))
+        stage = ctx.enter_context(tc.tile_pool(name="stage", bufs=4))
+        work = ctx.enter_context(tc.tile_pool(name="work", bufs=2))
+        psum = ctx.enter_context(tc.psum_pool(name="psum", bufs=8))
+
+        offsets = keep.tile([P, T // 16], U16, name="offsets")
+        nc.sync.dma_start(offsets[:], offs)
+
+        warm = keep.tile([P, 1], F32, name="warm")
+        nc.gpsimd.memset(warm[:], 0.0)
+        nc.scalar.activation(warm[:], warm[:], SIGMOID)
+
+        x_scales = keep.tile([P, T], U8, name="x_scales", align_bytes=64)
+        nc.gpsimd.memset(x_scales[:], 0)
+
+        def load(tile, src, cuts):
+            for lo, hi in zip(cuts[:-1], cuts[1:]):
+                nc.sync.dma_start(tile[:, :, lo:hi], src[:, :, lo:hi])
+
+        x_raw = []
+        for a in range(PASSES):
+            t = keep.tile([P, 4, T], F32, name=f"x_raw{a}")
+            load(t, xT[512 * a : 512 * a + 512, :].rearrange("(p j) w -> p j w", j=4), (0, 256, T) if a == 0 else (0, T))
+            x_raw.append(t)
+
+        w_raw = {}
+        w2_raw = {}
+        gates = keep.tile([P, BLOCKS, T], F32, name="gates")
+        gate_view = gate.rearrange("(b p) j -> p b j", p=P)
+
+        last_key = (E - 1, 1, PASSES - 1)
+        for e in range(E):
+            for which, w in ((0, w1), (1, w3)):
+                for a in range(PASSES):
+                    key = (e, which, a)
+                    t = keep.tile([P, 4, H], F32, name=f"w_raw{e}{which}{a}")
+                    src = w[e, 512 * a : 512 * a + 512, :].rearrange("(p j) c -> p j c", j=4)
+                    load(t, src, (0, 4 * LAST_CUT, H) if key == last_key else (0, H))
+                    w_raw[key] = t
+            t = keep.tile([P, 4, N], F32, name=f"w2_raw{e}")
+            nc.sync.dma_start(t[:], w2[e].rearrange("(p j) n -> p j n", j=4))
+            w2_raw[e] = t
+            nc.sync.dma_start(gates[:, :, C * e : C * e + C], gate_view[:, :, C * e : C * e + C])
+
+        def copy_on(engine, dst, src):
+            if engine == "S":
+                nc.scalar.copy(dst, src)
+            else:
+                nc.vector.tensor_copy(dst, src)
+
+        def interleave(grouped, raw, shares):
+            dst = grouped[:].rearrange("p (c i j) -> p c j i", i=4, j=4)
+            src = raw[:].rearrange("p j (c i) -> p c j i", i=4)
+            for engine, lo, hi in shares:
+                copy_on(engine, dst[:, lo // 4 : hi // 4], src[:, lo // 4 : hi // 4])
+
+        def interleave_permuted(grouped, raw, shares):
+            dst = grouped[:].rearrange("p (t m j) -> p m j t", t=4, j=4)
+            src = raw[:].rearrange("p j (m t) -> p m j t", t=4)
+            for engine, lo, hi in shares:
+                copy_on(engine, dst[:, lo:hi], src[:, lo:hi])
+
+        x_words, x_grouped = [], []
+
+        def x_inter(a):
+            g = stage.tile([P, 4 * T], BF16, name=f"x_grouped{a}", tag="grouped", align_bytes=64)
+            if a == 0:
+                shares = share(0, S_X[0] // 2, 256) + share(256, 256 + S_X[0] // 2, T)
+            else:
+                shares = share(0, S_X[a], T)
+            interleave(g, x_raw[a], shares)
+            x_grouped.append(g)
+
+        def x_quant(a):
+            t = keep.tile([P, T], U32, name=f"x_words{a}", align_bytes=64)
+            nc.vector.quantize_mx(out=t[:].bitcast(FP8X4), scales=x_scales[4 * a : P, :], in_=x_grouped[a][:])
+            x_words.append(t)
+
+        s_words = keep.tile([P, PASSES, E * C], U32, name="s_words", align_bytes=64)
+        s_scales = keep.tile([P, E * C], U8, name="s_scales", align_bytes=64)
+
+        def slot_list(lo, n):
+            return offsets[:, lo // 16 : (lo + n) // 16]
+
+        def gather_words(a, e):
+            nc.vector.tensor_copy(s_words[:, a, C * e : C * e + C], x_words[a][:].indirect(slot_list(C * e, C)))
+
+        def gather_scales(e):
+            nc.vector.tensor_copy(s_scales[:, C * e : C * e + C], x_scales[:].indirect(slot_list(C * e, C)))
+
+        w_grouped, w_codes, w_scales = {}, {}, {}
+
+        def w_inter(key):
+            e, which, a = key
+            g = stage.tile([P, 4 * H], BF16, name=f"w_grouped{e}{which}{a}", tag="grouped", align_bytes=64)
+            if key == last_key:
+                shares = share(0, LAST_S[0], LAST_CUT) + share(LAST_CUT, LAST_S[1], P)
+            else:
+                shares = share(0, S_WEIGHTS[2 * e + which][a], P)
+            interleave_permuted(g, w_raw[key], shares)
+            w_grouped[key] = g
+
+        def w_quant(key):
+            e, which, a = key
+            t = keep.tile([P, H], U32, name=f"w_codes{e}{which}{a}", align_bytes=64)
+            s = keep.tile([P, H], U8, name=f"w_scales{e}{which}{a}", align_bytes=64)
+            step = H // LAST_QUANTS if key == last_key else H
+            for lo in range(0, H, step):
+                nc.vector.quantize_mx(
+                    out=t[:, lo : lo + step].bitcast(FP8X4),
+                    scales=s[:, lo : lo + step],
+                    in_=w_grouped[key][:, 4 * lo : 4 * (lo + step)],
+                )
+            w_codes[key], w_scales[key] = t, s
+
+        w2_grouped, w2_codes, w2_scales = {}, {}, {}
+
+        def w2_inter(e):
+            g = stage.tile([P, 4 * N], BF16, name=f"w2_grouped{e}", tag="w2_grouped", bufs=2, align_bytes=64)
+            interleave(g, w2_raw[e], share(0, S_DOWN[e], N))
+            w2_grouped[e] = g
+
+        def w2_quant(e):
+            t = keep.tile([P, N], U32, name=f"w2_codes{e}", align_bytes=64)
+            s = keep.tile([P, N], U8, name=f"w2_scales{e}", align_bytes=64)
+            for lo, hi in ((0, 256), (256, N)):
+                nc.vector.quantize_mx(
+                    out=t[:, lo:hi].bitcast(FP8X4), scales=s[:, lo:hi], in_=w2_grouped[e][:, 4 * lo : 4 * hi]
+                )
+            w2_codes[e], w2_scales[e] = t, s
+
+        banks = {}
+
+        def first_layer(e, which, a):
+            slots = slice(C * e, C * e + C)
+            for t in range(4):
+                if a == 0:
+                    banks[(e, which, t)] = psum.tile([P, C], F32, name=f"bank{e}{which}{t}", tag="bank")
+                codes, scales = w_codes[(e, which, a)], w_scales[(e, which, a)]
+                nc.tensor.matmul_mx(
+                    out=banks[(e, which, t)][:],
+                    lhsT=codes[:, P * t : P * t + P].bitcast(FP8X4),
+                    lhsT_scale=scales[:, P * t : P * t + P],
+                    rhs=s_words[:, a, slots].bitcast(FP8X4),
+                    rhs_scale=s_scales[4 * a : P, slots],
+                    start=(a == 0),
+                    stop=(a == PASSES - 1),
+                )
+
+        sig, hid, hid_grouped, hid_codes = {}, {}, {}, {}
+
+        def sigmoid(e):
+            sig[e] = work.tile([P, 4, C], F32, name=f"sig{e}", tag="sig")
+            for t in range(4):
+                nc.scalar.activation(sig[e][:, t, :], banks[(e, 0, t)][:], SIGMOID)
+
+        def hidden(e):
+            hid[e] = work.tile([P, 4, C], BF16, name=f"hid{e}", tag="hid")
+            for t in range(4):
+                nc.vector.tensor_tensor(hid[e][:, t, :], banks[(e, 1, t)][:], sig[e][:, t, :], MULT)
+
+        def hidden_inter(e):
+            hid_grouped[e] = work.tile([P, C, 4], BF16, name=f"hid_grouped{e}", tag="hid_grouped", align_bytes=64)
+            for h in range(2):
+                slots = slice(HALF * h, HALF * h + HALF)
+                copy_on(
+                    HID_ENGINES[e][h],
+                    hid_grouped[e][:, slots, :],
+                    hid[e][:, :, slots].rearrange("p t n -> p n t"),
+                )
+
+        def hidden_quant(e):
+            t = work.tile([P, C], U32, name=f"hid_codes{e}", tag="hid_codes", align_bytes=64)
+            s = work.tile([P, C], U8, name=f"hid_scales{e}", tag="hid_scales", align_bytes=64)
+            for h in range(2):
+                slots = slice(HALF * h, HALF * h + HALF)
+                nc.vector.quantize_mx(
+                    out=t[:, slots].bitcast(FP8X4),
+                    scales=s[:, slots],
+                    in_=hid_grouped[e][:, slots, :].rearrange("p n t -> p (n t)"),
+                )
+            hid_codes[e] = (t, s)
+
+        y_slots = {}
+
+        def second_layer(e):
+            y_slots[e] = work.tile([P, BLOCKS, C], F32, name=f"y_slots{e}", tag="y_slots")
+            codes, scales = hid_codes[e]
+            for h in range(2):
+                slots = slice(HALF * h, HALF * h + HALF)
+                bank = psum.tile([P, BLOCKS, HALF], F32, name=f"y_bank{e}{h}", tag="bank")
+                for b in range(BLOCKS):
+                    nc.tensor.matmul_mx(
+                        out=bank[:, b, :],
+                        lhsT=w2_codes[e][:, P * b : P * b + P].bitcast(FP8X4),
+                        lhsT_scale=w2_scales[e][:, P * b : P * b + P],
+                        rhs=codes[:, slots].bitcast(FP8X4),
+                        rhs_scale=scales[:, slots],
+                        start=True,
+                        stop=True,
+                    )
+                nc.scalar.copy(y_slots[e][:, :, slots], bank[:])
+
+        windows = []
+        for b in range(BLOCKS):
+            t = keep.tile([P, T], F32, name=f"window{b}")
+            windows.append(t)
+
+        def scatter(e, b, lo, n):
+            first = C * e + lo
+            nc.vector.tensor_tensor(
+                windows[b][:].indirect(slot_list(first, n)),
+                y_slots[e][:, b, lo : lo + n],
+                gates[:, b, first : first + n],
+                MULT,
+            )
+
+        x_inter(0)
+        x_inter(1)
+        x_quant(0)
+        x_inter(2)
+        gather_words(0, 0)
+        x_quant(1)
+        gather_words(1, 0)
+        x_quant(2)
+        gather_words(2, 0)
+        gather_scales(0)
+
+        pieces = [(e, which, a) for e in range(E) for which in range(2) for a in range(PASSES)]
+        early = [(b, lo) for b in range(BLOCKS) for lo in range(0, C, SC0)]
+        w_inter(pieces[0])
+        for i, key in enumerate(pieces):
+            e, which, a = key
+            if i + 1 < len(pieces):
+                w_inter(pieces[i + 1])
+            if i == 5:
+                w2_inter(0)
+            w_quant(key)
+            if i < PASSES:
+                gather_words(i, 1)
+            if i == PASSES:
+                gather_scales(1)
+            first_layer(e, which, a)
+            if a == PASSES - 1:
+                if which == 0:
+                    sigmoid(e)
+                else:
+                    if e == 1:
+                        w2_inter(e)
+                    w2_quant(e)
+                    hidden(e)
+                    hidden_inter(e)
+                    hidden_quant(e)
+                    second_layer(e)
+            for q, (b, lo) in enumerate(early):
+                if SCATTER_AFTER[q] == i:
+                    scatter(0, b, lo, SC0)
+        for lo in range(0, C, SC1):
+            for b in range(BLOCKS):
+                scatter(1, b, lo, SC1)
+                if lo + SC1 == C:
+                    nc.sync.dma_start(out[P * b : P * b + P, :], windows[b][:])

@@ -18,16 +18,23 @@ P = 128
 PASSES = K // 512
 HALF = 128
 BLOCKS = N // P
-S_X = [208,272,480]
-S_WEIGHTS = [[96,16,72],[64,16,24],[88,104,128],[128,80,40]]
-S_DOWN = [256,256]
-LAST_CUT = 96
-LAST_S = [32,104]
-LAST_QUANTS = 1
-SCATTER_AFTER = [8,8,10]
-SC0 = 256
-SC1 = 256
-HID_ENGINES = [["V","S"],["V","S"]]
+S_X = [128,256,480]
+S_WEIGHTS = [[80,128,40],[128,16,104],[112,56,104],[128,56,88]]
+S_DOWN = [128,384]
+LAST_CUT = 64
+LAST_S = [64,88]
+LAST_QUANTS = 2
+SCATTER_AFTER = [5,10,8,10,10,5]
+FINE_Y = 1
+LOADS = [[0,0,0,0],[0,0,0,1],[0,0,0,2],[0,0,1,0],[0,0,1,1],[0,0,1,2],[2,0],[0,1,0,0],[3,0],[0,1,0,1],[0,1,0,2],[0,1,1,0],[3,1],[0,1,1,1],[0,1,1,2],[2,1]]
+SC0 = 128
+W2_AT = 0
+G1_AT = 2
+W2_LATE = 1
+Y_ENGINES = ["S","S"]
+BLOCK_FIRST = 0
+SC1 = 128
+HID_ENGINES = [["V","V"],["S","S"]]
 
 
 def share(lo, cut, hi):
@@ -38,7 +45,8 @@ def tile_routed_moe_kernel(tc, xT, w1, w3, w2, gate, offs, out):
     nc = tc.nc
     with ExitStack() as ctx:
         keep = ctx.enter_context(tc.tile_pool(name="keep", bufs=1))
-        stage = ctx.enter_context(tc.tile_pool(name="stage", bufs=4))
+        stage = ctx.enter_context(tc.tile_pool(name="stage", bufs=6))
+        wraw = ctx.enter_context(tc.tile_pool(name="wraw", bufs=9))
         work = ctx.enter_context(tc.tile_pool(name="work", bufs=2))
         psum = ctx.enter_context(tc.psum_pool(name="psum", bufs=8))
 
@@ -68,18 +76,20 @@ def tile_routed_moe_kernel(tc, xT, w1, w3, w2, gate, offs, out):
         gate_view = gate.rearrange("(b p) j -> p b j", p=P)
 
         last_key = (E - 1, 1, PASSES - 1)
-        for e in range(E):
-            for which, w in ((0, w1), (1, w3)):
-                for a in range(PASSES):
-                    key = (e, which, a)
-                    t = keep.tile([P, 4, H], F32, name=f"w_raw{e}{which}{a}")
-                    src = w[e, 512 * a : 512 * a + 512, :].rearrange("(p j) c -> p j c", j=4)
-                    load(t, src, (0, 4 * LAST_CUT, H) if key == last_key else (0, H))
-                    w_raw[key] = t
-            t = keep.tile([P, 4, N], F32, name=f"w2_raw{e}")
-            nc.sync.dma_start(t[:], w2[e].rearrange("(p j) n -> p j n", j=4))
-            w2_raw[e] = t
-            nc.sync.dma_start(gates[:, :, C * e : C * e + C], gate_view[:, :, C * e : C * e + C])
+        for kind, e, *rest in LOADS:
+            if kind == 0:
+                which, a = rest
+                key = (e, which, a)
+                t = wraw.tile([P, 4, H], F32, name=f"w_raw{e}{which}{a}", tag="w_raw")
+                src = (w1, w3)[which][e, 512 * a : 512 * a + 512, :].rearrange("(p j) c -> p j c", j=4)
+                load(t, src, (0, 4 * LAST_CUT, H) if key == last_key else (0, H))
+                w_raw[key] = t
+            elif kind == 2:
+                t = keep.tile([P, 4, N], F32, name=f"w2_raw{e}")
+                nc.sync.dma_start(t[:], w2[e].rearrange("(p j) n -> p j n", j=4))
+                w2_raw[e] = t
+            else:
+                nc.sync.dma_start(gates[:, :, C * e : C * e + C], gate_view[:, :, C * e : C * e + C])
 
         def copy_on(engine, dst, src):
             if engine == "S":
@@ -227,10 +237,14 @@ def tile_routed_moe_kernel(tc, xT, w1, w3, w2, gate, offs, out):
             codes, scales = hid_codes[e]
             for h in range(2):
                 slots = slice(HALF * h, HALF * h + HALF)
-                bank = psum.tile([P, BLOCKS, HALF], F32, name=f"y_bank{e}{h}", tag="bank")
+                fine = e == 1 and FINE_Y
                 for b in range(BLOCKS):
+                    if fine:
+                        bank = psum.tile([P, 1, HALF], F32, name=f"y_bank{e}{h}{b}", tag="bank")
+                    elif b == 0:
+                        bank = psum.tile([P, BLOCKS, HALF], F32, name=f"y_bank{e}{h}", tag="bank")
                     nc.tensor.matmul_mx(
-                        out=bank[:, b, :],
+                        out=bank[:, 0 if fine else b, :],
                         lhsT=w2_codes[e][:, P * b : P * b + P].bitcast(FP8X4),
                         lhsT_scale=w2_scales[e][:, P * b : P * b + P],
                         rhs=codes[:, slots].bitcast(FP8X4),
@@ -238,7 +252,10 @@ def tile_routed_moe_kernel(tc, xT, w1, w3, w2, gate, offs, out):
                         start=True,
                         stop=True,
                     )
-                nc.scalar.copy(y_slots[e][:, :, slots], bank[:])
+                    if fine:
+                        copy_on(Y_ENGINES[e], y_slots[e][:, b, slots], bank[:, 0, :])
+                if not fine:
+                    copy_on(Y_ENGINES[e], y_slots[e][:, :, slots], bank[:])
 
         windows = []
         for b in range(BLOCKS):
@@ -272,30 +289,36 @@ def tile_routed_moe_kernel(tc, xT, w1, w3, w2, gate, offs, out):
             e, which, a = key
             if i + 1 < len(pieces):
                 w_inter(pieces[i + 1])
-            if i == 5:
+            if i == W2_AT:
                 w2_inter(0)
             w_quant(key)
-            if i < PASSES:
-                gather_words(i, 1)
-            if i == PASSES:
+            if 0 <= i - G1_AT < PASSES:
+                gather_words(i - G1_AT, 1)
+            if i - G1_AT == PASSES:
                 gather_scales(1)
             first_layer(e, which, a)
             if a == PASSES - 1:
                 if which == 0:
                     sigmoid(e)
                 else:
-                    if e == 1:
-                        w2_inter(e)
-                    w2_quant(e)
+                    if e == 0 or W2_LATE == 0:
+                        if e == 1:
+                            w2_inter(e)
+                        w2_quant(e)
                     hidden(e)
                     hidden_inter(e)
+                    if e == 1 and W2_LATE == 1:
+                        w2_inter(e)
+                        w2_quant(e)
                     hidden_quant(e)
                     second_layer(e)
             for q, (b, lo) in enumerate(early):
                 if SCATTER_AFTER[q] == i:
                     scatter(0, b, lo, SC0)
-        for lo in range(0, C, SC1):
-            for b in range(BLOCKS):
-                scatter(1, b, lo, SC1)
-                if lo + SC1 == C:
-                    nc.sync.dma_start(out[P * b : P * b + P, :], windows[b][:])
+        final = [(b, lo) for lo in range(0, C, SC1) for b in range(BLOCKS)]
+        if BLOCK_FIRST:
+            final = [(b, lo) for b in range(BLOCKS) for lo in range(0, C, SC1)]
+        for b, lo in final:
+            scatter(1, b, lo, SC1)
+            if lo + SC1 == C:
+                nc.sync.dma_start(out[P * b : P * b + P, :], windows[b][:])

@@ -18,23 +18,29 @@ P = 128
 PASSES = K // 512
 HALF = 128
 BLOCKS = N // P
-S_X = [128,256,480]
-S_WEIGHTS = [[80,128,40],[128,16,104],[112,56,104],[128,56,88]]
-S_DOWN = [128,384]
+S_X = [128,320,480]
+S_WEIGHTS = [[128,112,128],[32,0,32],[128,48,128],[128,8,128]]
+S_DOWN = [128,256]
 LAST_CUT = 64
-LAST_S = [64,88]
-LAST_QUANTS = 2
-SCATTER_AFTER = [5,10,8,10,10,5]
+LAST_S = [32,64]
+LAST_QUANTS = 1
+SCATTER_AFTER = [7,9,10,9,9,5]
 FINE_Y = 1
-LOADS = [[0,0,0,0],[0,0,0,1],[0,0,0,2],[0,0,1,0],[0,0,1,1],[0,0,1,2],[2,0],[0,1,0,0],[3,0],[0,1,0,1],[0,1,0,2],[0,1,1,0],[3,1],[0,1,1,1],[0,1,1,2],[2,1]]
-SC0 = 128
-W2_AT = 0
-G1_AT = 2
+LOADS = [[0,0,0,0],[0,0,0,1],[0,0,0,2],[0,0,1,0],[0,0,1,1],[0,0,1,2],[2,0],[0,1,0,0],[0,1,0,1],[3,0],[0,1,0,2],[0,1,1,0],[3,1],[0,1,1,1],[0,1,1,2],[2,1]]
+FINALS = (
+    ((0, 0, 128), (1, 0, 128), (2, 0, 128), (0, 128, 128), (1, 128, 128), (2, 128, 128)),
+    ((0, 0, 128), (1, 0, 256), (2, 0, 256), (0, 128, 128)),
+    ((0, 0, 128), (1, 0, 128), (2, 0, 256), (0, 128, 128), (1, 128, 128)),
+    ((0, 0, 256), (1, 0, 256), (2, 0, 256)),
+)
+SC0 = 256
+W2_AT = 4
+G1_AT = 0
 W2_LATE = 1
 Y_ENGINES = ["S","S"]
-BLOCK_FIRST = 0
-SC1 = 128
-HID_ENGINES = [["V","V"],["S","S"]]
+BLOCK_FIRST = 1
+SC1 = 256
+HID_ENGINES = [["V","V"],["V","S"]]
 
 
 def share(lo, cut, hi):
@@ -315,10 +321,8 @@ def tile_routed_moe_kernel(tc, xT, w1, w3, w2, gate, offs, out):
             for q, (b, lo) in enumerate(early):
                 if SCATTER_AFTER[q] == i:
                     scatter(0, b, lo, SC0)
-        final = [(b, lo) for lo in range(0, C, SC1) for b in range(BLOCKS)]
-        if BLOCK_FIRST:
-            final = [(b, lo) for b in range(BLOCKS) for lo in range(0, C, SC1)]
-        for b, lo in final:
-            scatter(1, b, lo, SC1)
-            if lo + SC1 == C:
+        final = FINALS[BLOCK_FIRST]
+        for q, (b, lo, n) in enumerate(final):
+            scatter(1, b, lo, n)
+            if b not in [later[0] for later in final[q + 1 :]]:
                 nc.sync.dma_start(out[P * b : P * b + P, :], windows[b][:])

from contextlib import ExitStack

import concourse.mybir as mybir

K, T, E, C, H, N = 1536, 512, 2, 256, 512, 384
FLOPS = 2 * 2 * K * H * T + 2 * H * N * T

F32 = mybir.dt.float32
BF16 = mybir.dt.bfloat16
U32 = mybir.dt.uint32
U16 = mybir.dt.uint16
U8 = mybir.dt.uint8
FP8X4 = mybir.dt.float8_e4m3fn_x4
MULT = mybir.AluOpType.mult
SIGMOID = mybir.ActivationFunctionType.Sigmoid

P = 128
PASSES = K // 512
HALF = 128
BLOCKS = N // P
S_X = [128,320,480]
S_WEIGHTS = [[128,112,128],[32,0,32],[128,48,128],[128,8,128]]
S_DOWN = [128,256]
LAST_CUT = 64
LAST_S = [32,64]
LAST_QUANTS = 1
SCATTER_AFTER = [7,9,10,9,9,5]
FINE_Y = 1
LOADS = [[0,0,0,0],[0,0,0,1],[0,0,0,2],[0,0,1,0],[0,0,1,1],[0,0,1,2],[2,0],[0,1,0,0],[0,1,0,1],[3,0],[0,1,0,2],[0,1,1,0],[3,1],[0,1,1,1],[0,1,1,2],[2,1]]
FINALS = (
    ((0, 0, 128), (1, 0, 128), (2, 0, 128), (0, 128, 128), (1, 128, 128), (2, 128, 128)),
    ((0, 0, 128), (1, 0, 256), (2, 0, 256), (0, 128, 128)),
    ((0, 0, 128), (1, 0, 128), (2, 0, 256), (0, 128, 128), (1, 128, 128)),
    ((0, 0, 256), (1, 0, 256), (2, 0, 256)),
)
SC0 = 256
W2_AT = 4
G1_AT = 0
W2_LATE = 1
Y_ENGINES = ["S","S"]
BLOCK_FIRST = 1
SC1 = 256
HID_ENGINES = [["V","V"],["V","S"]]


def share(lo, cut, hi):
    return [(engine, a, b) for engine, a, b in (("S", lo, cut), ("V", cut, hi)) if a < b]


def tile_routed_moe_kernel(tc, xT, w1, w3, w2, gate, offs, out):
    nc = tc.nc
    with ExitStack() as ctx:
        keep = ctx.enter_context(tc.tile_pool(name="keep", bufs=1))
        stage = ctx.enter_context(tc.tile_pool(name="stage", bufs=6))
        wraw = ctx.enter_context(tc.tile_pool(name="wraw", bufs=9))
        work = ctx.enter_context(tc.tile_pool(name="work", bufs=2))
        psum = ctx.enter_context(tc.psum_pool(name="psum", bufs=8))

        offsets = keep.tile([P, T // 16], U16, name="offsets")
        nc.sync.dma_start(offsets[:], offs)

        warm = keep.tile([P, 1], F32, name="warm")
        nc.gpsimd.memset(warm[:], 0.0)
        nc.scalar.activation(warm[:], warm[:], SIGMOID)

        x_scales = keep.tile([P, T], U8, name="x_scales", align_bytes=64)
        nc.gpsimd.memset(x_scales[:], 0)

        def load(tile, src, cuts):
            for lo, hi in zip(cuts[:-1], cuts[1:]):
                nc.sync.dma_start(tile[:, :, lo:hi], src[:, :, lo:hi])

        x_raw = []
        for a in range(PASSES):
            t = keep.tile([P, 4, T], F32, name=f"x_raw{a}")
            load(t, xT[512 * a : 512 * a + 512, :].rearrange("(p j) w -> p j w", j=4), (0, 256, T) if a == 0 else (0, T))
            x_raw.append(t)

        w_raw = {}
        w2_raw = {}
        gates = keep.tile([P, BLOCKS, T], F32, name="gates")
        gate_view = gate.rearrange("(b p) j -> p b j", p=P)

        last_key = (E - 1, 1, PASSES - 1)
        for kind, e, *rest in LOADS:
            if kind == 0:
                which, a = rest
                key = (e, which, a)
                t = wraw.tile([P, 4, H], F32, name=f"w_raw{e}{which}{a}", tag="w_raw")
                src = (w1, w3)[which][e, 512 * a : 512 * a + 512, :].rearrange("(p j) c -> p j c", j=4)
                load(t, src, (0, 4 * LAST_CUT, H) if key == last_key else (0, H))
                w_raw[key] = t
            elif kind == 2:
                t = keep.tile([P, 4, N], F32, name=f"w2_raw{e}")
                nc.sync.dma_start(t[:], w2[e].rearrange("(p j) n -> p j n", j=4))
                w2_raw[e] = t
            else:
                nc.sync.dma_start(gates[:, :, C * e : C * e + C], gate_view[:, :, C * e : C * e + C])

        def copy_on(engine, dst, src):
            if engine == "S":
                nc.scalar.copy(dst, src)
            else:
                nc.vector.tensor_copy(dst, src)

        def interleave(grouped, raw, shares):
            dst = grouped[:].rearrange("p (c i j) -> p c j i", i=4, j=4)
            src = raw[:].rearrange("p j (c i) -> p c j i", i=4)
            for engine, lo, hi in shares:
                copy_on(engine, dst[:, lo // 4 : hi // 4], src[:, lo // 4 : hi // 4])

        def interleave_permuted(grouped, raw, shares):
            dst = grouped[:].rearrange("p (t m j) -> p m j t", t=4, j=4)
            src = raw[:].rearrange("p j (m t) -> p m j t", t=4)
            for engine, lo, hi in shares:
                copy_on(engine, dst[:, lo:hi], src[:, lo:hi])

        x_words, x_grouped = [], []

        def x_inter(a):
            g = stage.tile([P, 4 * T], BF16, name=f"x_grouped{a}", tag="grouped", align_bytes=64)
            if a == 0:
                shares = share(0, S_X[0] // 2, 256) + share(256, 256 + S_X[0] // 2, T)
            else:
                shares = share(0, S_X[a], T)
            interleave(g, x_raw[a], shares)
            x_grouped.append(g)

        def x_quant(a):
            t = keep.tile([P, T], U32, name=f"x_words{a}", align_bytes=64)
            nc.vector.quantize_mx(out=t[:].bitcast(FP8X4), scales=x_scales[4 * a : P, :], in_=x_grouped[a][:])
            x_words.append(t)

        s_words = keep.tile([P, PASSES, E * C], U32, name="s_words", align_bytes=64)
        s_scales = keep.tile([P, E * C], U8, name="s_scales", align_bytes=64)

        def slot_list(lo, n):
            return offsets[:, lo // 16 : (lo + n) // 16]

        def gather_words(a, e):
            nc.vector.tensor_copy(s_words[:, a, C * e : C * e + C], x_words[a][:].indirect(slot_list(C * e, C)))

        def gather_scales(e):
            nc.vector.tensor_copy(s_scales[:, C * e : C * e + C], x_scales[:].indirect(slot_list(C * e, C)))

        w_grouped, w_codes, w_scales = {}, {}, {}

        def w_inter(key):
            e, which, a = key
            g = stage.tile([P, 4 * H], BF16, name=f"w_grouped{e}{which}{a}", tag="grouped", align_bytes=64)
            if key == last_key:
                shares = share(0, LAST_S[0], LAST_CUT) + share(LAST_CUT, LAST_S[1], P)
            else:
                shares = share(0, S_WEIGHTS[2 * e + which][a], P)
            interleave_permuted(g, w_raw[key], shares)
            w_grouped[key] = g

        def w_quant(key):
            e, which, a = key
            t = keep.tile([P, H], U32, name=f"w_codes{e}{which}{a}", align_bytes=64)
            s = keep.tile([P, H], U8, name=f"w_scales{e}{which}{a}", align_bytes=64)
            step = H // LAST_QUANTS if key == last_key else H
            for lo in range(0, H, step):
                nc.vector.quantize_mx(
                    out=t[:, lo : lo + step].bitcast(FP8X4),
                    scales=s[:, lo : lo + step],
                    in_=w_grouped[key][:, 4 * lo : 4 * (lo + step)],
                )
            w_codes[key], w_scales[key] = t, s

        w2_grouped, w2_codes, w2_scales = {}, {}, {}

        def w2_inter(e):
            g = stage.tile([P, 4 * N], BF16, name=f"w2_grouped{e}", tag="w2_grouped", bufs=2, align_bytes=64)
            interleave(g, w2_raw[e], share(0, S_DOWN[e], N))
            w2_grouped[e] = g

        def w2_quant(e):
            t = keep.tile([P, N], U32, name=f"w2_codes{e}", align_bytes=64)
            s = keep.tile([P, N], U8, name=f"w2_scales{e}", align_bytes=64)
            for lo, hi in ((0, 256), (256, N)):
                nc.vector.quantize_mx(
                    out=t[:, lo:hi].bitcast(FP8X4), scales=s[:, lo:hi], in_=w2_grouped[e][:, 4 * lo : 4 * hi]
                )
            w2_codes[e], w2_scales[e] = t, s

        banks = {}

        def first_layer(e, which, a):
            slots = slice(C * e, C * e + C)
            for t in range(4):
                if a == 0:
                    banks[(e, which, t)] = psum.tile([P, C], F32, name=f"bank{e}{which}{t}", tag="bank")
                codes, scales = w_codes[(e, which, a)], w_scales[(e, which, a)]
                nc.tensor.matmul_mx(
                    out=banks[(e, which, t)][:],
                    lhsT=codes[:, P * t : P * t + P].bitcast(FP8X4),
                    lhsT_scale=scales[:, P * t : P * t + P],
                    rhs=s_words[:, a, slots].bitcast(FP8X4),
                    rhs_scale=s_scales[4 * a : P, slots],
                    start=(a == 0),
                    stop=(a == PASSES - 1),
                )

        sig, hid, hid_grouped, hid_codes = {}, {}, {}, {}

        def sigmoid(e):
            sig[e] = work.tile([P, 4, C], F32, name=f"sig{e}", tag="sig")
            for t in range(4):
                nc.scalar.activation(sig[e][:, t, :], banks[(e, 0, t)][:], SIGMOID)

        def hidden(e):
            hid[e] = work.tile([P, 4, C], BF16, name=f"hid{e}", tag="hid")
            for t in range(4):
                nc.vector.tensor_tensor(hid[e][:, t, :], banks[(e, 1, t)][:], sig[e][:, t, :], MULT)

        def hidden_inter(e):
            hid_grouped[e] = work.tile([P, C, 4], BF16, name=f"hid_grouped{e}", tag="hid_grouped", align_bytes=64)
            for h in range(2):
                slots = slice(HALF * h, HALF * h + HALF)
                copy_on(
                    HID_ENGINES[e][h],
                    hid_grouped[e][:, slots, :],
                    hid[e][:, :, slots].rearrange("p t n -> p n t"),
                )

        def hidden_quant(e):
            t = work.tile([P, C], U32, name=f"hid_codes{e}", tag="hid_codes", align_bytes=64)
            s = work.tile([P, C], U8, name=f"hid_scales{e}", tag="hid_scales", align_bytes=64)
            for h in range(2):
                slots = slice(HALF * h, HALF * h + HALF)
                nc.vector.quantize_mx(
                    out=t[:, slots].bitcast(FP8X4),
                    scales=s[:, slots],
                    in_=hid_grouped[e][:, slots, :].rearrange("p n t -> p (n t)"),
                )
            hid_codes[e] = (t, s)

        y_slots = {}

        def second_layer(e):
            y_slots[e] = work.tile([P, BLOCKS, C], F32, name=f"y_slots{e}", tag="y_slots")
            codes, scales = hid_codes[e]
            for h in range(2):
                slots = slice(HALF * h, HALF * h + HALF)
                fine = e == 1 and FINE_Y
                for b in range(BLOCKS):
                    if fine:
                        bank = psum.tile([P, 1, HALF], F32, name=f"y_bank{e}{h}{b}", tag="bank")
                    elif b == 0:
                        bank = psum.tile([P, BLOCKS, HALF], F32, name=f"y_bank{e}{h}", tag="bank")
                    nc.tensor.matmul_mx(
                        out=bank[:, 0 if fine else b, :],
                        lhsT=w2_codes[e][:, P * b : P * b + P].bitcast(FP8X4),
                        lhsT_scale=w2_scales[e][:, P * b : P * b + P],
                        rhs=codes[:, slots].bitcast(FP8X4),
                        rhs_scale=scales[:, slots],
                        start=True,
                        stop=True,
                    )
                    if fine:
                        copy_on(Y_ENGINES[e], y_slots[e][:, b, slots], bank[:, 0, :])
                if not fine:
                    copy_on(Y_ENGINES[e], y_slots[e][:, :, slots], bank[:])

        windows = []
        for b in range(BLOCKS):
            t = keep.tile([P, T], F32, name=f"window{b}")
            windows.append(t)

        def scatter(e, b, lo, n):
            first = C * e + lo
            nc.vector.tensor_tensor(
                windows[b][:].indirect(slot_list(first, n)),
                y_slots[e][:, b, lo : lo + n],
                gates[:, b, first : first + n],
                MULT,
            )

        x_inter(0)
        x_inter(1)
        x_quant(0)
        x_inter(2)
        gather_words(0, 0)
        x_quant(1)
        gather_words(1, 0)
        x_quant(2)
        gather_words(2, 0)
        gather_scales(0)

        pieces = [(e, which, a) for e in range(E) for which in range(2) for a in range(PASSES)]
        early = [(b, lo) for b in range(BLOCKS) for lo in range(0, C, SC0)]
        w_inter(pieces[0])
        for i, key in enumerate(pieces):
            e, which, a = key
            if i + 1 < len(pieces):
                w_inter(pieces[i + 1])
            if i == W2_AT:
                w2_inter(0)
            w_quant(key)
            if 0 <= i - G1_AT < PASSES:
                gather_words(i - G1_AT, 1)
            if i - G1_AT == PASSES:
                gather_scales(1)
            first_layer(e, which, a)
            if a == PASSES - 1:
                if which == 0:
                    sigmoid(e)
                else:
                    if e == 0 or W2_LATE == 0:
                        if e == 1:
                            w2_inter(e)
                        w2_quant(e)
                    hidden(e)
                    hidden_inter(e)
                    if e == 1 and W2_LATE == 1:
                        w2_inter(e)
                        w2_quant(e)
                    hidden_quant(e)
                    second_layer(e)
            for q, (b, lo) in enumerate(early):
                if SCATTER_AFTER[q] == i:
                    scatter(0, b, lo, SC0)
        final = FINALS[BLOCK_FIRST]
        for q, (b, lo, n) in enumerate(final):
            scatter(1, b, lo, n)
            if b not in [later[0] for later in final[q + 1 :]]:
                nc.sync.dma_start(out[P * b : P * b + P, :], windows[b][:])
